import numpy as np
import ml_dtypes


def mxq(x, axis, fmt="e4m3"):
    dtype, down = {"e4m3": (ml_dtypes.float8_e4m3fn, 7), "e5m2": (ml_dtypes.float8_e5m2, 14)}[fmt]
    v = np.moveaxis(np.asarray(x, np.float32).astype(ml_dtypes.bfloat16).astype(np.float64), axis, -1)
    blocks = v.reshape(v.shape[:-1] + (-1, 32))
    amax = np.abs(blocks).max(-1, keepdims=True)
    byte = np.maximum(np.where(amax > 0, np.frexp(amax)[1] - 1 + 127, 0) - down, 1)
    scale = np.exp2(byte - 127.0)
    codes = (blocks / scale).astype(np.float32).astype(dtype).astype(np.float64)
    return np.moveaxis((codes * scale).reshape(v.shape), -1, axis)


WIDE = False


def mx_kscale(k):
    if not WIDE:
        return np.ones(k)
    levels = np.array([10, -10, 5, -5, 0])
    if k % 512:
        return np.exp2(np.random.permutation(np.resize(levels, k // 32))).repeat(32)
    a = np.empty((k // 512, 16))
    for p in range(k // 512):
        a[p, :8] = np.random.permutation(np.resize(levels, 8))
        for g in range(8):
            far = levels[np.abs(levels - a[p, g]) >= 10]
            a[p, g + 8] = far[np.random.randint(len(far))]
    return np.exp2(a.ravel()).repeat(32)


BF16 = ml_dtypes.bfloat16


def bf(x):
    return np.asarray(x, np.float32).astype(BF16)


def f64(x):
    return np.asarray(x).astype(np.float64)


T, L, H, DK, DV = 2048, 512, 8, 128, 256


def draw0():
    s = mx_kscale(L)
    u = mx_kscale(T)
    r = 2.0 / T ** 0.25
    return {"c": bf(np.random.standard_normal((T, L)) * s),
            "wk": bf(np.random.standard_normal((L, H * DK)) / np.sqrt(L) / s[:, None]),
            "wv": bf(np.random.standard_normal((L, H * DV)) / np.sqrt(L) / s[:, None]),
            "keep": bf(np.random.uniform(0.5, 1.0, (T, H)) * r * u[:, None]),
            "write": bf(np.random.uniform(0.5, 1.5, (T, H)) * r / u[:, None])}


def core(c, wk, wv, keep, write):
    cq = mxq(f64(c), 1, "e4m3")
    k = np.maximum(cq @ mxq(f64(wk), 0, "e4m3"), 0.0)
    k = k.reshape(T, H, DK) * f64(keep)[:, :, None]
    v = cq @ mxq(f64(wv), 0, "e4m3")
    v = v.reshape(T, H, DV) * f64(write)[:, :, None]
    kq = mxq(k, 0, "e4m3").transpose(1, 2, 0)
    vq = mxq(v, 0, "e4m3").transpose(1, 0, 2)
    return kq @ vq


def e4m3fn_bytes(y):
    return np.clip(np.asarray(y, np.float64), -448.0, 448.0).astype(np.float32).astype(ml_dtypes.float8_e4m3fn).view(np.uint8)


def e4m3fn_values(b):
    return np.asarray(b, np.uint8).view(ml_dtypes.float8_e4m3fn).astype(np.float64)


def setup_inputs():
    d = draw0()
    x0 = np.asarray(d['wv']).astype(np.float64)
    s = (np.max(np.abs(x0), axis=(1,), keepdims=True) / 448.0).astype(np.float32)
    out = {}
    for k, v in d.items():
        if k == 'wv':
            out['wv_bytes'] = e4m3fn_bytes(x0 / s.astype(np.float64))
            out['wv_scale'] = s
        else:
            out[k] = v
    return out


def reference(c, wk, wv_bytes, wv_scale, keep, write):
    return core(c, wk, e4m3fn_values(wv_bytes) * wv_scale.astype(np.float64), keep, write)

@@ -1,0 +1,359 @@
+from contextlib import ExitStack
+
+import concourse.mybir as mybir
+from concourse.masks import make_identity
+
+F32 = mybir.dt.float32
+BF16 = mybir.dt.bfloat16
+U32 = mybir.dt.uint32
+U8 = mybir.dt.uint8
+FP8 = mybir.dt.float8_e4m3fn
+FP8X4 = mybir.dt.float8_e4m3fn_x4
+ALU = mybir.AluOpType
+COPY = mybir.ActivationFunctionType.Copy
+
+T, L, H, DK, DV = 2048, 512, 8, 128, 256
+P = 128
+G = 4
+FLOPS = 2 * T * L * H * (DK + DV) + 2 * T * H * DK * DV
+
+UNITS = H * G
+MODES = "WWAAWVWWVWWAVWVAWWWVAWWWAVWWVAWA"
+WK_ENG = "s"
+WV_ENG = "s"
+ACC = 6
+ACS = 0
+WID_ENG = "vvvs"
+WID0 = "vvvv"
+C0 = "ss"
+OB = 1
+WB = 1
+LW1 = 1
+LW2 = 2
+LQ = 5
+LF = 3
+LEAD = 7
+COUT = "vs"
+
+
+def tile_latent_kv_state_s7_kernel(tc, c, wk, wv_bytes, wv_scale, keep, write, out):
+    nc = tc.nc
+    with ExitStack() as ctx:
+        const = ctx.enter_context(tc.tile_pool(name="const", bufs=1))
+        stage = ctx.enter_context(tc.tile_pool(name="stage", bufs=3))
+        psum = ctx.enter_context(tc.psum_pool(name="psum", bufs=1))
+
+        ident = const.tile([P, P], F32, name="ident")
+        ident_b = const.tile([P, P], BF16, name="ident_b")
+        c_sb = const.tile([P, G, 4, L], BF16, name="c_sb", align_bytes=64)
+        wk_raw = const.tile([P, 4, H * DK], BF16, name="wk_raw", align_bytes=64)
+        wv_raw = const.tile([P, 4, H * DV], U8, name="wv_raw", align_bytes=64)
+        wvs = const.tile([P, 4], F32, name="wvs")
+        kp_raw = const.tile([P, G, 32], BF16, name="kp_raw")
+        wr_raw = const.tile([P, G, 32], BF16, name="wr_raw")
+        kp = const.tile([P, G, H, 4], F32, name="kp")
+        wr = const.tile([P, G, H, 4], F32, name="wr")
+        c_cod = const.tile([P, G, 512], U32, name="c_cod", align_bytes=64)
+        c_scl = const.tile([P, G, 512], U8, name="c_scl", align_bytes=64)
+        wk_cod = const.tile([P, H, DK], U32, name="wk_cod", align_bytes=64)
+        wk_scl = const.tile([P, H, DK], U8, name="wk_scl", align_bytes=64)
+        wv_cod = const.tile([P, H, DV], U32, name="wv_cod", align_bytes=64)
+        wv_scl = const.tile([P, H, DV], U8, name="wv_scl", align_bytes=64)
+        warm = const.tile([P, 1], F32, name="warm")
+
+        ctx.enter_context(tc.manual_schedule())
+
+        wv_view = wv_bytes.rearrange("(p j) w -> p j w", j=4)
+        wk_view = wk.rearrange("(p j) w -> p j w", j=4)
+        c_view = c.rearrange("(g p t) l -> g p t l", p=P, t=4)
+
+        nc.scalar.dma_start(out=wvs[:], in_=wv_scale.rearrange("(p j) o -> p (j o)", j=4))
+        nc.scalar.dma_start(out=wr_raw[:], in_=write.rearrange("(g p t) h -> p g (t h)", p=P, t=4))
+        nc.scalar.dma_start(out=kp_raw[:], in_=keep.rearrange("(g p t) h -> p g (t h)", p=P, t=4))
+
+        def load_wv(a, b):
+            nc.sync.dma_start(out=wv_raw[:, :, a * DV : b * DV], in_=wv_view[:, :, a * DV : b * DV])
+
+        def load_wk(a, b):
+            nc.sync.dma_start(out=wk_raw[:, :, a * DK : b * DK], in_=wk_view[:, :, a * DK : b * DK])
+
+        def load_c(g):
+            nc.sync.dma_start(out=c_sb[:, g, :, :], in_=c_view[g])
+
+        load_wv(0, 1)
+        load_c(0)
+        load_wk(0, 2)
+        load_c(1)
+        load_wv(1, 4)
+        load_c(2)
+        load_c(3)
+        load_wk(2, 8)
+        load_wv(4, 8)
+
+        make_identity(nc, ident[:])
+        nc.gpsimd.tensor_copy(out=ident_b[:], in_=ident[:])
+        nc.vector.memset(warm[:], 0.0)
+        nc.scalar.activation(out=warm[:], in_=warm[:], func=COPY)
+
+        def interleave(engine, dst, src):
+            d4 = dst.rearrange("p (c i) t -> p c t i", i=4)
+            s4 = src.rearrange("p t (c i) -> p c t i", i=4)
+            if engine == "g":
+                nc.gpsimd.tensor_scalar(out=d4, in0=s4, scalar1=1.0, scalar2=0.0, op0=ALU.mult, op1=ALU.add)
+            elif engine == "s":
+                nc.scalar.copy(out=d4, in_=s4)
+            else:
+                nc.vector.tensor_copy(out=d4, in_=s4)
+
+        wide = {}
+        vgrp = {}
+        kgrp = {}
+
+        def widen(h):
+            w = stage.tile([P, 4, DV], BF16, name="wv_wide", bufs=2)
+            wide[h] = w
+            for j in range(4):
+                raw = wv_raw[:, j, h * DV : (h + 1) * DV].bitcast(FP8)
+                if (WID_ENG if h else WID0)[j] == "s":
+                    nc.scalar.activation(out=w[:, j, :], in_=raw, func=COPY, scale=wvs[:, j : j + 1])
+                else:
+                    nc.vector.tensor_scalar(out=w[:, j, :], in0=raw, scalar1=wvs[:, j : j + 1], scalar2=None, op0=ALU.mult)
+
+        def group_wv(h, engine):
+            t = stage.tile([P, DV, 4], BF16, name="wv_grp", bufs=2, align_bytes=64)
+            vgrp[h] = t
+            interleave(engine, t[:], wide.pop(h)[:])
+
+        def group_wk(h, engine):
+            t = stage.tile([P, DK, 4], BF16, name="wk_grp", bufs=2, align_bytes=64)
+            kgrp[h] = t
+            interleave(engine, t[:], wk_raw[:, :, h * DK : (h + 1) * DK])
+
+        def quant_w(h):
+            nc.vector.quantize_mx(
+                out=wv_cod[:, h, :].bitcast(FP8X4), scales=wv_scl[:, h, :], in_=vgrp.pop(h)[:].rearrange("p n t -> p (n t)")
+            )
+            nc.vector.quantize_mx(
+                out=wk_cod[:, h, :].bitcast(FP8X4), scales=wk_scl[:, h, :], in_=kgrp.pop(h)[:].rearrange("p n t -> p (n t)")
+            )
+
+        xt = {}
+        cgrp = {}
+
+        def transpose_c(g):
+            words = c_sb[:, g, :, :].bitcast(F32)
+            for b in range(2):
+                bank = psum.tile([P, 2, 2, P], F32, name="acc", bufs=ACC)
+                xt[g, b] = bank
+                for i in range(2):
+                    for u in range(2):
+                        nc.tensor.transpose(bank[:, i, u, :], words[:, 2 * b + i, u::2], ident[:])
+
+        def c_out(g, engines):
+            t = stage.tile([P, 2, 2, P, 4], BF16, name="c_grp", bufs=2, align_bytes=64)
+            cgrp[g] = t
+            for b in range(2):
+                dst = t[:, b, :, :, :].bitcast(F32)
+                src = xt.pop((g, b))[:].rearrange("q i u r -> q i r u")
+                if engines[b] == "s":
+                    nc.scalar.copy(out=dst, in_=src)
+                else:
+                    nc.vector.tensor_copy(out=dst, in_=src)
+
+        def quant_c(g):
+            nc.vector.quantize_mx(
+                out=c_cod[:, g, :].bitcast(FP8X4),
+                scales=c_scl[:, g, :],
+                in_=cgrp.pop(g)[:].rearrange("q b i r e -> q (b i r e)"),
+            )
+
+        kbank = {}
+        vbank = {}
+
+        def mm(out_ap, g, t, cod, scl):
+            nc.tensor.matmul_mx(
+                out=out_ap,
+                lhsT=c_cod[:, g, t * P : (t + 1) * P].bitcast(FP8X4),
+                lhsT_scale=c_scl[:, g, t * P : (t + 1) * P],
+                rhs=cod.bitcast(FP8X4),
+                rhs_scale=scl,
+                start=True,
+                stop=True,
+            )
+
+        def project(s):
+            h, g = s // G, s % G
+            bank = psum.tile([P, 4, P], F32, name="acc", bufs=ACC)
+            kbank[s] = bank
+            for t in range(4):
+                mm(bank[:, t, :], g, t, wk_cod[:, h, :], wk_scl[:, h, :])
+            if MODES[s] == "A":
+                for f in range(2):
+                    bank = psum.tile([P, 4, P], F32, name="acc", bufs=ACC)
+                    vbank[s, f] = bank
+                    for t in range(4):
+                        cols = slice(f * P, (f + 1) * P)
+                        mm(bank[:, t, :], g, t, wv_cod[:, h, cols], wv_scl[:, h, cols])
+            else:
+                for f in range(2):
+                    if ACS:
+                        bank = psum.tile([P, 2, DV], F32, name="acs", bufs=ACS)
+                    else:
+                        bank = psum.tile([P, 2, DV], F32, name="acc", bufs=ACC)
+                    vbank[s, f] = bank
+                    for i in range(2):
+                        mm(bank[:, i, :], g, 2 * f + i, wv_cod[:, h, :], wv_scl[:, h, :])
+
+        kin = {}
+        vin = {}
+        vt = {}
+        kcod = {}
+        vcod = {}
+
+        def ins(s):
+            if s // 2 not in kin:
+                k_in = stage.tile([P, 2, DK, 4], BF16, name="k_in", align_bytes=64)
+                v_in = stage.tile([P, 2, DV, 4], BF16, name="v_in", align_bytes=64)
+                kin[s // 2] = k_in
+                vin[s // 2] = v_in
+
+        def key(s):
+            h, g = s // G, s % G
+            ins(s)
+            nc.vector.scalar_tensor_tensor(
+                out=kin[s // 2][:, s % 2, :, :],
+                in0=kbank.pop(s)[:].rearrange("p t n -> p n t"),
+                scalar=0.0,
+                in1=kp[:, g, h, :].unsqueeze(1).to_broadcast([P, DK, 4]),
+                op0=ALU.max,
+                op1=ALU.mult,
+            )
+
+        def val_direct(s):
+            h, g = s // G, s % G
+            ins(s)
+            for f in range(2):
+                nc.vector.tensor_tensor(
+                    out=vin[s // 2][:, s % 2, f * P : (f + 1) * P, :],
+                    in0=vbank.pop((s, f))[:].rearrange("p t n -> p n t"),
+                    in1=wr[:, g, h, :].unsqueeze(1).to_broadcast([P, P, 4]),
+                    op=ALU.mult,
+                )
+
+        def val_scalar(s):
+            h, g = s // G, s % G
+            v_t = stage.tile([P, 4, DV], BF16, name="v_t", align_bytes=64)
+            vt[s] = v_t
+            for t in range(4):
+                nc.scalar.activation(
+                    out=v_t[:, t, :], in_=vbank[s, t // 2][:, t % 2, :], func=COPY, scale=wr[:, g, h, t : t + 1]
+                )
+
+        def val_group(s):
+            ins(s)
+            interleave("g" if MODES[s] == "G" else "v", vin[s // 2][:, s % 2, :, :], vt.pop(s)[:])
+
+        wbank = {}
+
+        def weave(s):
+            bank = psum.tile([P, DV, 4], BF16, name="w_acc", bufs=WB)
+            wbank[s] = bank
+            src = vt.pop(s)[:].rearrange("p t n -> p n t")
+            for f in range(2):
+                cols = slice(f * P, (f + 1) * P)
+                nc.tensor.matmul(out=bank[:, cols, :], lhsT=ident_b[:], rhs=src[:, cols, :], start=True, stop=True)
+
+        def weave_out(s):
+            ins(s)
+            nc.scalar.copy(out=vin[s // 2][:, s % 2, :, :], in_=wbank.pop(s)[:])
+
+        def quant_kv(p):
+            kc = stage.tile([P, 2, DK], U32, name="k_cod", bufs=5, align_bytes=64)
+            ks = stage.tile([P, 2, DK], U8, name="k_scl", bufs=5, align_bytes=64)
+            vc = stage.tile([P, 2, DV], U32, name="v_cod", bufs=5, align_bytes=64)
+            vs = stage.tile([P, 2, DV], U8, name="v_scl", bufs=5, align_bytes=64)
+            kcod[p] = (kc, ks)
+            vcod[p] = (vc, vs)
+            nc.vector.quantize_mx(
+                out=kc[:].rearrange("p a n -> p (a n)").bitcast(FP8X4),
+                scales=ks[:].rearrange("p a n -> p (a n)"),
+                in_=kin.pop(p)[:].rearrange("p a n t -> p (a n t)"),
+            )
+            nc.vector.quantize_mx(
+                out=vc[:].rearrange("p a n -> p (a n)").bitcast(FP8X4),
+                scales=vs[:].rearrange("p a n -> p (a n)"),
+                in_=vin.pop(p)[:].rearrange("p a n t -> p (a n t)"),
+            )
+
+        obank = {}
+
+        def fold(h):
+            bank = psum.tile([P, DV], F32, name="o_acc", bufs=OB)
+            obank[h] = bank
+            for g in range(G):
+                (kc, ks), (vc, vs) = kcod[2 * h + g // 2], vcod[2 * h + g // 2]
+                nc.tensor.matmul_mx(
+                    out=bank[:],
+                    lhsT=kc[:, g % 2, :].bitcast(FP8X4),
+                    lhsT_scale=ks[:, g % 2, :],
+                    rhs=vc[:, g % 2, :].bitcast(FP8X4),
+                    rhs_scale=vs[:, g % 2, :],
+                    start=(g == 0),
+                    stop=(g == G - 1),
+                )
+
+        def store(h):
+            o = stage.tile([P, DV], F32, name="o_sb", bufs=2)
+            nc.scalar.copy(out=o[:], in_=obank.pop(h)[:])
+            nc.sync.dma_start(out=out[h], in_=o[:])
+
+        widen(0)
+        group_wv(0, "v")
+        transpose_c(0)
+        c_out(0, C0)
+        group_wk(0, "v")
+        quant_w(0)
+        quant_c(0)
+        nc.vector.tensor_copy(out=wr[:], in_=wr_raw[:].rearrange("p g (t h) -> p g h t", t=4))
+        nc.vector.tensor_copy(out=kp[:], in_=kp_raw[:].rearrange("p g (t h) -> p g h t", t=4))
+        transpose_c(1)
+        c_out(1, COUT)
+
+        for s in range(UNITS + LQ + LF + 2):
+            u = s - LF - LQ - 2
+            if 0 <= u < 4 * H and u % 4 == 0:
+                fold(u // 4)
+            if s < UNITS:
+                project(s)
+            if s + 2 < 4:
+                transpose_c(s + 2)
+            if 0 <= s - LW1 < UNITS and MODES[s - LW1] == "W":
+                weave(s - LW1)
+            if s < UNITS and MODES[s] != "A":
+                val_scalar(s)
+            if 0 <= s - LW2 < UNITS and MODES[s - LW2] == "W":
+                weave_out(s - LW2)
+            if s < 3:
+                quant_c(s + 1)
+            if s >= LQ and (s - LQ) % 2 == 0 and s - LQ < UNITS:
+                quant_kv((s - LQ) // 2)
+            if s < UNITS:
+                key(s)
+                if MODES[s] == "A":
+                    val_direct(s)
+            if 0 <= s - LW1 < UNITS and MODES[s - LW1] in "VG":
+                val_group(s - LW1)
+            if s + 2 < 4:
+                c_out(s + 2, COUT)
+            for h1 in range(1, H):
+                first = max(0, 4 * h1 - LEAD)
+                if s == first:
+                    widen(h1)
+                    group_wk(h1, WK_ENG)
+                elif s == first + 1:
+                    group_wv(h1, WV_ENG)
+                elif s == first + 2:
+                    quant_w(h1)
+            u = s - LF - LQ - 3
+            if 0 <= u < 4 * H and u % 4 == 0:
+                store(u // 4)

@@ -18,21 +18,21 @@ G = 4
 FLOPS = 2 * T * L * H * (DK + DV) + 2 * T * H * DK * DV
 
 UNITS = H * G
-MODES = "WWAAWVWWVWWAVWVAWWWVAWWWAVWWVAWA"
+MODES = "VAVVVVVVVVVVVVVVVVVVVVVVVVVVVVVV"
 WK_ENG = "s"
 WV_ENG = "s"
 ACC = 6
 ACS = 0
-WID_ENG = "vvvs"
-WID0 = "vvvv"
+WID_ENG = "ssss"
+WID0 = "svvv"
 C0 = "ss"
 OB = 1
 WB = 1
 LW1 = 1
 LW2 = 2
-LQ = 5
+LQ = 3
 LF = 3
-LEAD = 7
+LEAD = 5
 COUT = "vs"
 
 

@@ -18,29 +18,36 @@ G = 4
 FLOPS = 2 * T * L * H * (DK + DV) + 2 * T * H * DK * DV
 
 UNITS = H * G
-MODES = "VAVVVVVVVVVVVVVVVVVVVVVVVVVVVVVV"
+MODES = "AAAAPPPAPPAPAPPAPPPPAAPAPPPPPPAP"
 WK_ENG = "s"
 WV_ENG = "s"
-ACC = 6
+ACC = 7
+SB = 6
+GROUPS = [[0,2],[2,4],[4,6],[6,8]]
+WK0 = "s"
+LOADS = "v02 c0 k02 c1 c2 c3 v28 k28"
+WV0 = "v"
+C0FIRST = False
+PG = 0
 ACS = 0
 WID_ENG = "ssss"
-WID0 = "svvv"
+WID0 = "vsvs"
 C0 = "ss"
 OB = 1
 WB = 1
 LW1 = 1
 LW2 = 2
-LQ = 3
-LF = 3
-LEAD = 5
-COUT = "vs"
+LQ = 5
+LF = 2
+LEAD = 6
+COUT = "ss"
 
 
 def tile_latent_kv_state_s7_kernel(tc, c, wk, wv_bytes, wv_scale, keep, write, out):
     nc = tc.nc
     with ExitStack() as ctx:
         const = ctx.enter_context(tc.tile_pool(name="const", bufs=1))
-        stage = ctx.enter_context(tc.tile_pool(name="stage", bufs=3))
+        stage = ctx.enter_context(tc.tile_pool(name="stage", bufs=SB))
         psum = ctx.enter_context(tc.psum_pool(name="psum", bufs=1))
 
         ident = const.tile([P, P], F32, name="ident")
@@ -80,15 +87,13 @@ def tile_latent_kv_state_s7_kernel(tc, c, wk, wv_bytes, wv_scale, keep, write, o
         def load_c(g):
             nc.sync.dma_start(out=c_sb[:, g, :, :], in_=c_view[g])
 
-        load_wv(0, 1)
-        load_c(0)
-        load_wk(0, 2)
-        load_c(1)
-        load_wv(1, 4)
-        load_c(2)
-        load_c(3)
-        load_wk(2, 8)
-        load_wv(4, 8)
+        for item in LOADS.split():
+            if item[0] == "c":
+                load_c(int(item[1]))
+            elif item[0] == "k":
+                load_wk(int(item[1]), int(item[2]))
+            else:
+                load_wv(int(item[1]), int(item[2]))
 
         make_identity(nc, ident[:])
         nc.gpsimd.tensor_copy(out=ident_b[:], in_=ident[:])
@@ -109,32 +114,41 @@ def tile_latent_kv_state_s7_kernel(tc, c, wk, wv_bytes, wv_scale, keep, write, o
         vgrp = {}
         kgrp = {}
 
-        def widen(h):
-            w = stage.tile([P, 4, DV], BF16, name="wv_wide", bufs=2)
-            wide[h] = w
-            for j in range(4):
-                raw = wv_raw[:, j, h * DV : (h + 1) * DV].bitcast(FP8)
-                if (WID_ENG if h else WID0)[j] == "s":
-                    nc.scalar.activation(out=w[:, j, :], in_=raw, func=COPY, scale=wvs[:, j : j + 1])
+        def widen(a, b, js, engs):
+            if a not in wide:
+                w = stage.tile([P, 4, (b - a) * DV], BF16, name="wv_wide", bufs=2)
+                wide[a] = w
+            for j in js:
+                raw = wv_raw[:, j, a * DV : b * DV].bitcast(FP8)
+                if engs[j] == "s":
+                    nc.scalar.activation(out=wide[a][:, j, :], in_=raw, func=COPY, scale=wvs[:, j : j + 1])
                 else:
-                    nc.vector.tensor_scalar(out=w[:, j, :], in0=raw, scalar1=wvs[:, j : j + 1], scalar2=None, op0=ALU.mult)
+                    nc.vector.tensor_scalar(out=wide[a][:, j, :], in0=raw, scalar1=wvs[:, j : j + 1], scalar2=None, op0=ALU.mult)
 
-        def group_wv(h, engine):
-            t = stage.tile([P, DV, 4], BF16, name="wv_grp", bufs=2, align_bytes=64)
-            vgrp[h] = t
-            interleave(engine, t[:], wide.pop(h)[:])
+        def group_wv(a, b, engs):
+            t = stage.tile([P, (b - a) * DV, 4], BF16, name="wv_grp", bufs=2, align_bytes=64)
+            vgrp[a] = t
+            n = (b - a) * DV // len(engs)
+            for i in range(len(engs)):
+                interleave(engs[i], t[:, i * n : (i + 1) * n, :], wide[a][:, :, i * n : (i + 1) * n])
 
-        def group_wk(h, engine):
-            t = stage.tile([P, DK, 4], BF16, name="wk_grp", bufs=2, align_bytes=64)
-            kgrp[h] = t
-            interleave(engine, t[:], wk_raw[:, :, h * DK : (h + 1) * DK])
+        def group_wk(a, b, engine):
+            t = stage.tile([P, (b - a) * DK, 4], BF16, name="wk_grp", bufs=2, align_bytes=64)
+            kgrp[a] = t
+            interleave(engine, t[:], wk_raw[:, :, a * DK : b * DK])
 
-        def quant_w(h):
+        def quant_wv(a, b):
             nc.vector.quantize_mx(
-                out=wv_cod[:, h, :].bitcast(FP8X4), scales=wv_scl[:, h, :], in_=vgrp.pop(h)[:].rearrange("p n t -> p (n t)")
+                out=wv_cod[:, a:b, :].rearrange("p h n -> p (h n)").bitcast(FP8X4),
+                scales=wv_scl[:, a:b, :].rearrange("p h n -> p (h n)"),
+                in_=vgrp.pop(a)[:].rearrange("p n t -> p (n t)"),
             )
+
+        def quant_wk(a, b):
             nc.vector.quantize_mx(
-                out=wk_cod[:, h, :].bitcast(FP8X4), scales=wk_scl[:, h, :], in_=kgrp.pop(h)[:].rearrange("p n t -> p (n t)")
+                out=wk_cod[:, a:b, :].rearrange("p h n -> p (h n)").bitcast(FP8X4),
+                scales=wk_scl[:, a:b, :].rearrange("p h n -> p (h n)"),
+                in_=kgrp.pop(a)[:].rearrange("p n t -> p (n t)"),
             )
 
         xt = {}
@@ -246,11 +260,20 @@ def tile_latent_kv_state_s7_kernel(tc, c, wk, wv_bytes, wv_scale, keep, write, o
             vt[s] = v_t
             for t in range(4):
                 nc.scalar.activation(
-                    out=v_t[:, t, :], in_=vbank[s, t // 2][:, t % 2, :], func=COPY, scale=wr[:, g, h, t : t + 1]
+                    out=v_t[:, t, :] if MODES[s] != "P" else v_t[:].rearrange("p t n -> p (t n)").rearrange("p (q n e) -> p q n e", q=2, e=2)[:, t // 2, :, t % 2],
+                    in_=vbank[s, t // 2][:, t % 2, :], func=COPY, scale=wr[:, g, h, t : t + 1]
                 )
 
         def val_group(s):
             ins(s)
+            if MODES[s] == "P":
+                src = vt.pop(s)[:].rearrange("p t n -> p (t n)").bitcast(F32).rearrange("p (q n) -> p n q", q=2)
+                dst = vin[s // 2][:, s % 2, :, :].bitcast(F32)
+                if PG and s % PG == 0:
+                    nc.gpsimd.tensor_scalar(out=dst, in0=src, scalar1=1.0, scalar2=0.0, op0=ALU.mult, op1=ALU.add)
+                else:
+                    nc.vector.tensor_copy(out=dst, in_=src)
+                return
             interleave("g" if MODES[s] == "G" else "v", vin[s // 2][:, s % 2, :, :], vt.pop(s)[:])
 
         wbank = {}
@@ -258,10 +281,11 @@ def tile_latent_kv_state_s7_kernel(tc, c, wk, wv_bytes, wv_scale, keep, write, o
         def weave(s):
             bank = psum.tile([P, DV, 4], BF16, name="w_acc", bufs=WB)
             wbank[s] = bank
-            src = vt.pop(s)[:].rearrange("p t n -> p n t")
+            src = vt.pop(s)[:]
+            dst = bank[:].rearrange("p n t -> p t n")
             for f in range(2):
-                cols = slice(f * P, (f + 1) * P)
-                nc.tensor.matmul(out=bank[:, cols, :], lhsT=ident_b[:], rhs=src[:, cols, :], start=True, stop=True)
+                cols = slice(2 * f, 2 * f + 2)
+                nc.tensor.matmul(out=dst[:, cols, :], lhsT=ident_b[:], rhs=src[:, cols, :], start=True, stop=True)
 
         def weave_out(s):
             ins(s)
@@ -307,12 +331,17 @@ def tile_latent_kv_state_s7_kernel(tc, c, wk, wv_bytes, wv_scale, keep, write, o
             nc.scalar.copy(out=o[:], in_=obank.pop(h)[:])
             nc.sync.dma_start(out=out[h], in_=o[:])
 
-        widen(0)
-        group_wv(0, "v")
+        ga, gb = GROUPS[0]
+        widen(ga, gb, range(4), WID0)
         transpose_c(0)
-        c_out(0, C0)
-        group_wk(0, "v")
-        quant_w(0)
+        if C0FIRST:
+            c_out(0, C0)
+        group_wv(ga, gb, WV0)
+        group_wk(ga, gb, WK0)
+        if not C0FIRST:
+            c_out(0, C0)
+        quant_wv(ga, gb)
+        quant_wk(ga, gb)
         quant_c(0)
         nc.vector.tensor_copy(out=wr[:], in_=wr_raw[:].rearrange("p g (t h) -> p g h t", t=4))
         nc.vector.tensor_copy(out=kp[:], in_=kp_raw[:].rearrange("p g (t h) -> p g h t", t=4))
@@ -341,19 +370,22 @@ def tile_latent_kv_state_s7_kernel(tc, c, wk, wv_bytes, wv_scale, keep, write, o
                 key(s)
                 if MODES[s] == "A":
                     val_direct(s)
-            if 0 <= s - LW1 < UNITS and MODES[s - LW1] in "VG":
+            if 0 <= s - LW1 < UNITS and MODES[s - LW1] in "VGP":
                 val_group(s - LW1)
             if s + 2 < 4:
                 c_out(s + 2, COUT)
-            for h1 in range(1, H):
-                first = max(0, 4 * h1 - LEAD)
+            for a, b in GROUPS[1:]:
+                first = max(0, 4 * a - LEAD)
                 if s == first:
-                    widen(h1)
-                    group_wk(h1, WK_ENG)
+                    widen(a, b, (0, 1), WID_ENG)
+                    group_wk(a, b, WK_ENG)
                 elif s == first + 1:
-                    group_wv(h1, WV_ENG)
+                    widen(a, b, (2, 3), WID_ENG)
+                    quant_wk(a, b)
                 elif s == first + 2:
-                    quant_w(h1)
+                    group_wv(a, b, WV_ENG)
+                elif s == first + 3:
+                    quant_wv(a, b)
             u = s - LF - LQ - 3
             if 0 <= u < 4 * H and u % 4 == 0:
                 store(u // 4)

@@ -18,28 +18,31 @@ G = 4
 FLOPS = 2 * T * L * H * (DK + DV) + 2 * T * H * DK * DV
 
 UNITS = H * G
-MODES = "AAAAPPPAPPAPAPPAPPPPAAPAPPPPPPAP"
+MODES = "AAGAGAGAPAGPAGGAGAGAGAGPPAGPPAPP"
 WK_ENG = "s"
-WV_ENG = "s"
-ACC = 7
+WV_ENG = "ss"
+ACC = 5
 SB = 6
-GROUPS = [[0,2],[2,4],[4,6],[6,8]]
+GROUPS = [[0,1],[1,2],[2,3],[3,4],[4,5],[5,6],[6,7],[7,8]]
 WK0 = "s"
-LOADS = "v02 c0 k02 c1 c2 c3 v28 k28"
-WV0 = "v"
+LOADS = "c0 v01 k01 c1 v12 k12 c2 c3 v24 k24 v48 k48"
+WV0 = "vs"
 C0FIRST = False
 PG = 0
-ACS = 0
+ACS = 2
 WID_ENG = "ssss"
 WID0 = "vsvs"
-C0 = "ss"
+C0 = "sv"
 OB = 1
 WB = 1
 LW1 = 1
 LW2 = 2
-LQ = 5
-LF = 2
-LEAD = 6
+LQ = 2
+LF = 3
+LO = 1
+LI = 1
+HOLD = True
+LEAD = 3
 COUT = "ss"
 
 
@@ -334,12 +337,9 @@ def tile_latent_kv_state_s7_kernel(tc, c, wk, wv_bytes, wv_scale, keep, write, o
         ga, gb = GROUPS[0]
         widen(ga, gb, range(4), WID0)
         transpose_c(0)
-        if C0FIRST:
-            c_out(0, C0)
         group_wv(ga, gb, WV0)
         group_wk(ga, gb, WK0)
-        if not C0FIRST:
-            c_out(0, C0)
+        c_out(0, C0)
         quant_wv(ga, gb)
         quant_wk(ga, gb)
         quant_c(0)
@@ -347,45 +347,59 @@ def tile_latent_kv_state_s7_kernel(tc, c, wk, wv_bytes, wv_scale, keep, write, o
         nc.vector.tensor_copy(out=kp[:], in_=kp_raw[:].rearrange("p g (t h) -> p g h t", t=4))
         transpose_c(1)
         c_out(1, COUT)
+        quant_c(1)
 
-        for s in range(UNITS + LQ + LF + 2):
-            u = s - LF - LQ - 2
-            if 0 <= u < 4 * H and u % 4 == 0:
-                fold(u // 4)
-            if s < UNITS:
-                project(s)
-            if s + 2 < 4:
-                transpose_c(s + 2)
-            if 0 <= s - LW1 < UNITS and MODES[s - LW1] == "W":
-                weave(s - LW1)
-            if s < UNITS and MODES[s] != "A":
-                val_scalar(s)
-            if 0 <= s - LW2 < UNITS and MODES[s - LW2] == "W":
-                weave_out(s - LW2)
-            if s < 3:
-                quant_c(s + 1)
-            if s >= LQ and (s - LQ) % 2 == 0 and s - LQ < UNITS:
-                quant_kv((s - LQ) // 2)
-            if s < UNITS:
-                key(s)
-                if MODES[s] == "A":
-                    val_direct(s)
-            if 0 <= s - LW1 < UNITS and MODES[s - LW1] in "VGP":
-                val_group(s - LW1)
-            if s + 2 < 4:
-                c_out(s + 2, COUT)
+        def hold(p):
+            mark = stage.tile([P, 1], U32, name="mark", bufs=2)
+            nc.gpsimd.tensor_copy(out=mark[:], in_=vcod[p][0][:, 1, DV - 1 : DV])
+
+        PAIRS = UNITS // 2
+        for p in range(PAIRS + 8):
+            u = p - LF
+            if 0 <= u < PAIRS and u % 2 == 1:
+                fold(u // 2)
+            if p < PAIRS:
+                project(2 * p)
+                project(2 * p + 1)
+                if p == 0:
+                    transpose_c(2)
+                    transpose_c(3)
+                for s in (2 * p, 2 * p + 1):
+                    if MODES[s] != "A":
+                        val_scalar(s)
+            if 0 <= p - LQ < PAIRS:
+                quant_kv(p - LQ)
             for a, b in GROUPS[1:]:
-                first = max(0, 4 * a - LEAD)
-                if s == first:
-                    widen(a, b, (0, 1), WID_ENG)
+                first = 2 * a - LEAD
+                if p == max(0, first):
+                    widen(a, b, range(4), WID_ENG)
                     group_wk(a, b, WK_ENG)
-                elif s == first + 1:
-                    widen(a, b, (2, 3), WID_ENG)
-                    quant_wk(a, b)
-                elif s == first + 2:
+                if p == max(0, first + 1):
                     group_wv(a, b, WV_ENG)
-                elif s == first + 3:
+                    quant_wk(a, b)
+                if p == max(0, first + 2):
                     quant_wv(a, b)
-            u = s - LF - LQ - 3
-            if 0 <= u < 4 * H and u % 4 == 0:
-                store(u // 4)
+            if 0 <= p - LI < PAIRS:
+                for s in (2 * (p - LI), 2 * (p - LI) + 1):
+                    if MODES[s] in "VP":
+                        val_group(s)
+            if 0 <= p - LI < PAIRS:
+                for s in (2 * (p - LI), 2 * (p - LI) + 1):
+                    if MODES[s] == "G":
+                        if HOLD and 0 <= p - LQ < PAIRS:
+                            hold(p - LQ)
+                        val_group(s)
+            if p < PAIRS:
+                for s in (2 * p, 2 * p + 1):
+                    key(s)
+                for s in (2 * p, 2 * p + 1):
+                    if MODES[s] == "A":
+                        val_direct(s)
+                if p == 0:
+                    c_out(2, COUT)
+                    c_out(3, COUT)
+                    quant_c(2)
+                    quant_c(3)
+            u = p - LF - LO
+            if 0 <= u < PAIRS and u % 2 == 1:
+                store(u // 2)

@@ -18,22 +18,22 @@ G = 4
 FLOPS = 2 * T * L * H * (DK + DV) + 2 * T * H * DK * DV
 
 UNITS = H * G
-MODES = "AAGAGAGAPAGPAGGAGAGAGAGPPAGPPAPP"
+MODES = "GAGAAGGPPAPGAGPGGGGAGAPGPGPGPGAP"
 WK_ENG = "s"
-WV_ENG = "ss"
-ACC = 5
+WV_ENG = "vs"
+ACC = 6
 SB = 6
-GROUPS = [[0,1],[1,2],[2,3],[3,4],[4,5],[5,6],[6,7],[7,8]]
-WK0 = "s"
-LOADS = "c0 v01 k01 c1 v12 k12 c2 c3 v24 k24 v48 k48"
-WV0 = "vs"
+GROUPS = ((0, 1), (1, 2), (2, 4), (4, 6), (6, 8))
+WK0 = "v"
+LOADS = "v01 c0 k01 c1 c2 v12 k12 c3 v24 k24 v48 k48"
+WV0 = "v"
 C0FIRST = False
 PG = 0
-ACS = 2
+ACS = 0
 WID_ENG = "ssss"
-WID0 = "vsvs"
+WID0 = "ssss"
 C0 = "sv"
-OB = 1
+OB = 2
 WB = 1
 LW1 = 1
 LW2 = 2
@@ -42,8 +42,12 @@ LF = 3
 LO = 1
 LI = 1
 HOLD = True
-LEAD = 3
-COUT = "ss"
+WARM = 6
+HW = 2
+KKAA = False
+HEAD = ["wd:0:vsvs","iv:0:v","ik:0:s","t:0","t:1","qv:0","o:0:vs","qk:0","t:2","o:1:vs","q:0","q:1","p:0","cv:0","o:2:ss","p:1","a:0","k:0","s:1","t:3","q:2","s:0","p:2","o:3:ss","a:1","k:1","wd:1:ssss","g:0","k:2","ik:1:s","q:3","g:1","p:3","z:0","iv:1:vs","s:2","qk:1","qv:1","a:3","k:3","a:2","s:3"]
+LEAD = 4
+COUT = "sv"
 
 
 def tile_latent_kv_state_s7_kernel(tc, c, wk, wv_bytes, wv_scale, keep, write, out):
@@ -70,6 +74,7 @@ def tile_latent_kv_state_s7_kernel(tc, c, wk, wv_bytes, wv_scale, keep, write, o
         wv_cod = const.tile([P, H, DV], U32, name="wv_cod", align_bytes=64)
         wv_scl = const.tile([P, H, DV], U8, name="wv_scl", align_bytes=64)
         warm = const.tile([P, 1], F32, name="warm")
+        zero = const.tile([P, 512], BF16, name="zero")
 
         ctx.enter_context(tc.manual_schedule())
 
@@ -100,6 +105,7 @@ def tile_latent_kv_state_s7_kernel(tc, c, wk, wv_bytes, wv_scale, keep, write, o
 
         make_identity(nc, ident[:])
         nc.gpsimd.tensor_copy(out=ident_b[:], in_=ident[:])
+        nc.vector.memset(zero[:], 0.0)
         nc.vector.memset(warm[:], 0.0)
         nc.scalar.activation(out=warm[:], in_=warm[:], func=COPY)
 
@@ -107,7 +113,7 @@ def tile_latent_kv_state_s7_kernel(tc, c, wk, wv_bytes, wv_scale, keep, write, o
             d4 = dst.rearrange("p (c i) t -> p c t i", i=4)
             s4 = src.rearrange("p t (c i) -> p c t i", i=4)
             if engine == "g":
-                nc.gpsimd.tensor_scalar(out=d4, in0=s4, scalar1=1.0, scalar2=0.0, op0=ALU.mult, op1=ALU.add)
+                nc.gpsimd.tensor_scalar(out=dst, in0=src.rearrange("p t n -> p n t"), scalar1=1.0, scalar2=0.0, op0=ALU.mult, op1=ALU.add)
             elif engine == "s":
                 nc.scalar.copy(out=d4, in_=s4)
             else:
@@ -334,72 +340,107 @@ def tile_latent_kv_state_s7_kernel(tc, c, wk, wv_bytes, wv_scale, keep, write, o
             nc.scalar.copy(out=o[:], in_=obank.pop(h)[:])
             nc.sync.dma_start(out=out[h], in_=o[:])
 
-        ga, gb = GROUPS[0]
-        widen(ga, gb, range(4), WID0)
-        transpose_c(0)
-        group_wv(ga, gb, WV0)
-        group_wk(ga, gb, WK0)
-        c_out(0, C0)
-        quant_wv(ga, gb)
-        quant_wk(ga, gb)
-        quant_c(0)
-        nc.vector.tensor_copy(out=wr[:], in_=wr_raw[:].rearrange("p g (t h) -> p g h t", t=4))
-        nc.vector.tensor_copy(out=kp[:], in_=kp_raw[:].rearrange("p g (t h) -> p g h t", t=4))
-        transpose_c(1)
-        c_out(1, COUT)
-        quant_c(1)
-
         def hold(p):
             mark = stage.tile([P, 1], U32, name="mark", bufs=2)
             nc.gpsimd.tensor_copy(out=mark[:], in_=vcod[p][0][:, 1, DV - 1 : DV])
 
         PAIRS = UNITS // 2
-        for p in range(PAIRS + 8):
+        if WARM:
+            bank = psum.tile([P, 512], F32, name="o_acc", bufs=OB)
+            for i in range(WARM):
+                nc.tensor.matmul(out=bank[:], lhsT=zero[:, :P], rhs=zero[:], start=True, stop=True)
+
+        def scales():
+            nc.vector.tensor_copy(out=wr[:], in_=wr_raw[:].rearrange("p g (t h) -> p g h t", t=4))
+            nc.vector.tensor_copy(out=kp[:], in_=kp_raw[:].rearrange("p g (t h) -> p g h t", t=4))
+
+        for item in HEAD:
+            f = item.split(":")
+            i = int(f[1])
+            if f[0] == "wd":
+                widen(i, i + 1, range(4), f[2])
+            elif f[0] == "iv":
+                group_wv(i, i + 1, f[2])
+            elif f[0] == "ik":
+                group_wk(i, i + 1, f[2])
+            elif f[0] == "qv":
+                quant_wv(i, i + 1)
+            elif f[0] == "qk":
+                quant_wk(i, i + 1)
+            elif f[0] == "t":
+                transpose_c(i)
+            elif f[0] == "o":
+                c_out(i, f[2])
+            elif f[0] == "q":
+                quant_c(i)
+            elif f[0] == "cv":
+                scales()
+            elif f[0] == "p":
+                project(i)
+            elif f[0] == "s":
+                if MODES[i] != "A":
+                    val_scalar(i)
+            elif f[0] == "k":
+                key(i)
+            elif f[0] == "a":
+                if MODES[i] == "A":
+                    val_direct(i)
+            elif f[0] == "g":
+                if MODES[i] in "VPG":
+                    val_group(i)
+            elif f[0] == "z":
+                quant_kv(i)
+
+        for p in range(2, PAIRS + 8):
             u = p - LF
             if 0 <= u < PAIRS and u % 2 == 1:
                 fold(u // 2)
-            if p < PAIRS:
-                project(2 * p)
-                project(2 * p + 1)
-                if p == 0:
-                    transpose_c(2)
-                    transpose_c(3)
-                for s in (2 * p, 2 * p + 1):
-                    if MODES[s] != "A":
-                        val_scalar(s)
-            if 0 <= p - LQ < PAIRS:
+            gjobs = []
+            if 1 <= p - LQ < PAIRS:
                 quant_kv(p - LQ)
-            for a, b in GROUPS[1:]:
+            for a in range(HW, H):
                 first = 2 * a - LEAD
-                if p == max(0, first):
+                b = a + 1
+                if p == max(2, first):
                     widen(a, b, range(4), WID_ENG)
                     group_wk(a, b, WK_ENG)
-                if p == max(0, first + 1):
-                    group_wv(a, b, WV_ENG)
+                if p == max(2, first + 1):
+                    if WV_ENG == "g":
+                        gjobs.append((group_wv, a, b))
+                    else:
+                        group_wv(a, b, WV_ENG)
                     quant_wk(a, b)
-                if p == max(0, first + 2):
+                if p == max(2, first + 2):
                     quant_wv(a, b)
-            if 0 <= p - LI < PAIRS:
-                for s in (2 * (p - LI), 2 * (p - LI) + 1):
+            if 1 <= p - 1 < PAIRS:
+                for s in (2 * (p - 1), 2 * (p - 1) + 1):
                     if MODES[s] in "VP":
                         val_group(s)
-            if 0 <= p - LI < PAIRS:
-                for s in (2 * (p - LI), 2 * (p - LI) + 1):
-                    if MODES[s] == "G":
-                        if HOLD and 0 <= p - LQ < PAIRS:
-                            hold(p - LQ)
-                        val_group(s)
+                    elif MODES[s] == "G":
+                        gjobs.append((val_group, s))
+            if gjobs and 1 <= p - LQ < PAIRS:
+                hold(p - LQ)
+            for job in gjobs:
+                if job[0] is val_group:
+                    val_group(job[1])
+                else:
+                    job[0](job[1], job[2], "g")
             if p < PAIRS:
                 for s in (2 * p, 2 * p + 1):
-                    key(s)
-                for s in (2 * p, 2 * p + 1):
-                    if MODES[s] == "A":
-                        val_direct(s)
-                if p == 0:
-                    c_out(2, COUT)
-                    c_out(3, COUT)
-                    quant_c(2)
-                    quant_c(3)
+                    project(s)
+                    if MODES[s] != "A":
+                        val_scalar(s)
+                if KKAA:
+                    key(2 * p)
+                    key(2 * p + 1)
+                    for s in (2 * p, 2 * p + 1):
+                        if MODES[s] == "A":
+                            val_direct(s)
+                else:
+                    for s in (2 * p, 2 * p + 1):
+                        key(s)
+                        if MODES[s] == "A":
+                            val_direct(s)
             u = p - LF - LO
             if 0 <= u < PAIRS and u % 2 == 1:
                 store(u // 2)

from contextlib import ExitStack

import concourse.mybir as mybir
from concourse.masks import make_identity

F32 = mybir.dt.float32
BF16 = mybir.dt.bfloat16
U32 = mybir.dt.uint32
U8 = mybir.dt.uint8
FP8 = mybir.dt.float8_e4m3fn
FP8X4 = mybir.dt.float8_e4m3fn_x4
ALU = mybir.AluOpType
COPY = mybir.ActivationFunctionType.Copy

T, L, H, DK, DV = 2048, 512, 8, 128, 256
P = 128
G = 4
FLOPS = 2 * T * L * H * (DK + DV) + 2 * T * H * DK * DV

UNITS = H * G
MODES = "GAGAAGGPPAPGAGPGGGGAGAPGPGPGPGAP"
WK_ENG = "s"
WV_ENG = "vs"
ACC = 6
SB = 6
GROUPS = ((0, 1), (1, 2), (2, 4), (4, 6), (6, 8))
WK0 = "v"
LOADS = "v01 c0 k01 c1 c2 v12 k12 c3 v24 k24 v48 k48"
WV0 = "v"
C0FIRST = False
PG = 0
ACS = 0
WID_ENG = "ssss"
WID0 = "ssss"
C0 = "sv"
OB = 2
WB = 1
LW1 = 1
LW2 = 2
LQ = 2
LF = 3
LO = 1
LI = 1
HOLD = True
WARM = 6
HW = 2
KKAA = False
HEAD = ["wd:0:vsvs","iv:0:v","ik:0:s","t:0","t:1","qv:0","o:0:vs","qk:0","t:2","o:1:vs","q:0","q:1","p:0","cv:0","o:2:ss","p:1","a:0","k:0","s:1","t:3","q:2","s:0","p:2","o:3:ss","a:1","k:1","wd:1:ssss","g:0","k:2","ik:1:s","q:3","g:1","p:3","z:0","iv:1:vs","s:2","qk:1","qv:1","a:3","k:3","a:2","s:3"]
LEAD = 4
COUT = "sv"


def tile_latent_kv_state_s7_kernel(tc, c, wk, wv_bytes, wv_scale, keep, write, out):
    nc = tc.nc
    with ExitStack() as ctx:
        const = ctx.enter_context(tc.tile_pool(name="const", bufs=1))
        stage = ctx.enter_context(tc.tile_pool(name="stage", bufs=SB))
        psum = ctx.enter_context(tc.psum_pool(name="psum", bufs=1))

        ident = const.tile([P, P], F32, name="ident")
        ident_b = const.tile([P, P], BF16, name="ident_b")
        c_sb = const.tile([P, G, 4, L], BF16, name="c_sb", align_bytes=64)
        wk_raw = const.tile([P, 4, H * DK], BF16, name="wk_raw", align_bytes=64)
        wv_raw = const.tile([P, 4, H * DV], U8, name="wv_raw", align_bytes=64)
        wvs = const.tile([P, 4], F32, name="wvs")
        kp_raw = const.tile([P, G, 32], BF16, name="kp_raw")
        wr_raw = const.tile([P, G, 32], BF16, name="wr_raw")
        kp = const.tile([P, G, H, 4], F32, name="kp")
        wr = const.tile([P, G, H, 4], F32, name="wr")
        c_cod = const.tile([P, G, 512], U32, name="c_cod", align_bytes=64)
        c_scl = const.tile([P, G, 512], U8, name="c_scl", align_bytes=64)
        wk_cod = const.tile([P, H, DK], U32, name="wk_cod", align_bytes=64)
        wk_scl = const.tile([P, H, DK], U8, name="wk_scl", align_bytes=64)
        wv_cod = const.tile([P, H, DV], U32, name="wv_cod", align_bytes=64)
        wv_scl = const.tile([P, H, DV], U8, name="wv_scl", align_bytes=64)
        warm = const.tile([P, 1], F32, name="warm")
        zero = const.tile([P, 512], BF16, name="zero")

        ctx.enter_context(tc.manual_schedule())

        wv_view = wv_bytes.rearrange("(p j) w -> p j w", j=4)
        wk_view = wk.rearrange("(p j) w -> p j w", j=4)
        c_view = c.rearrange("(g p t) l -> g p t l", p=P, t=4)

        nc.scalar.dma_start(out=wvs[:], in_=wv_scale.rearrange("(p j) o -> p (j o)", j=4))
        nc.scalar.dma_start(out=wr_raw[:], in_=write.rearrange("(g p t) h -> p g (t h)", p=P, t=4))
        nc.scalar.dma_start(out=kp_raw[:], in_=keep.rearrange("(g p t) h -> p g (t h)", p=P, t=4))

        def load_wv(a, b):
            nc.sync.dma_start(out=wv_raw[:, :, a * DV : b * DV], in_=wv_view[:, :, a * DV : b * DV])

        def load_wk(a, b):
            nc.sync.dma_start(out=wk_raw[:, :, a * DK : b * DK], in_=wk_view[:, :, a * DK : b * DK])

        def load_c(g):
            nc.sync.dma_start(out=c_sb[:, g, :, :], in_=c_view[g])

        for item in LOADS.split():
            if item[0] == "c":
                load_c(int(item[1]))
            elif item[0] == "k":
                load_wk(int(item[1]), int(item[2]))
            else:
                load_wv(int(item[1]), int(item[2]))

        make_identity(nc, ident[:])
        nc.gpsimd.tensor_copy(out=ident_b[:], in_=ident[:])
        nc.vector.memset(zero[:], 0.0)
        nc.vector.memset(warm[:], 0.0)
        nc.scalar.activation(out=warm[:], in_=warm[:], func=COPY)

        def interleave(engine, dst, src):
            d4 = dst.rearrange("p (c i) t -> p c t i", i=4)
            s4 = src.rearrange("p t (c i) -> p c t i", i=4)
            if engine == "g":
                nc.gpsimd.tensor_scalar(out=dst, in0=src.rearrange("p t n -> p n t"), scalar1=1.0, scalar2=0.0, op0=ALU.mult, op1=ALU.add)
            elif engine == "s":
                nc.scalar.copy(out=d4, in_=s4)
            else:
                nc.vector.tensor_copy(out=d4, in_=s4)

        wide = {}
        vgrp = {}
        kgrp = {}

        def widen(a, b, js, engs):
            if a not in wide:
                w = stage.tile([P, 4, (b - a) * DV], BF16, name="wv_wide", bufs=2)
                wide[a] = w
            for j in js:
                raw = wv_raw[:, j, a * DV : b * DV].bitcast(FP8)
                if engs[j] == "s":
                    nc.scalar.activation(out=wide[a][:, j, :], in_=raw, func=COPY, scale=wvs[:, j : j + 1])
                else:
                    nc.vector.tensor_scalar(out=wide[a][:, j, :], in0=raw, scalar1=wvs[:, j : j + 1], scalar2=None, op0=ALU.mult)

        def group_wv(a, b, engs):
            t = stage.tile([P, (b - a) * DV, 4], BF16, name="wv_grp", bufs=2, align_bytes=64)
            vgrp[a] = t
            n = (b - a) * DV // len(engs)
            for i in range(len(engs)):
                interleave(engs[i], t[:, i * n : (i + 1) * n, :], wide[a][:, :, i * n : (i + 1) * n])

        def group_wk(a, b, engine):
            t = stage.tile([P, (b - a) * DK, 4], BF16, name="wk_grp", bufs=2, align_bytes=64)
            kgrp[a] = t
            interleave(engine, t[:], wk_raw[:, :, a * DK : b * DK])

        def quant_wv(a, b):
            nc.vector.quantize_mx(
                out=wv_cod[:, a:b, :].rearrange("p h n -> p (h n)").bitcast(FP8X4),
                scales=wv_scl[:, a:b, :].rearrange("p h n -> p (h n)"),
                in_=vgrp.pop(a)[:].rearrange("p n t -> p (n t)"),
            )

        def quant_wk(a, b):
            nc.vector.quantize_mx(
                out=wk_cod[:, a:b, :].rearrange("p h n -> p (h n)").bitcast(FP8X4),
                scales=wk_scl[:, a:b, :].rearrange("p h n -> p (h n)"),
                in_=kgrp.pop(a)[:].rearrange("p n t -> p (n t)"),
            )

        xt = {}
        cgrp = {}

        def transpose_c(g):
            words = c_sb[:, g, :, :].bitcast(F32)
            for b in range(2):
                bank = psum.tile([P, 2, 2, P], F32, name="acc", bufs=ACC)
                xt[g, b] = bank
                for i in range(2):
                    for u in range(2):
                        nc.tensor.transpose(bank[:, i, u, :], words[:, 2 * b + i, u::2], ident[:])

        def c_out(g, engines):
            t = stage.tile([P, 2, 2, P, 4], BF16, name="c_grp", bufs=2, align_bytes=64)
            cgrp[g] = t
            for b in range(2):
                dst = t[:, b, :, :, :].bitcast(F32)
                src = xt.pop((g, b))[:].rearrange("q i u r -> q i r u")
                if engines[b] == "s":
                    nc.scalar.copy(out=dst, in_=src)
                else:
                    nc.vector.tensor_copy(out=dst, in_=src)

        def quant_c(g):
            nc.vector.quantize_mx(
                out=c_cod[:, g, :].bitcast(FP8X4),
                scales=c_scl[:, g, :],
                in_=cgrp.pop(g)[:].rearrange("q b i r e -> q (b i r e)"),
            )

        kbank = {}
        vbank = {}

        def mm(out_ap, g, t, cod, scl):
            nc.tensor.matmul_mx(
                out=out_ap,
                lhsT=c_cod[:, g, t * P : (t + 1) * P].bitcast(FP8X4),
                lhsT_scale=c_scl[:, g, t * P : (t + 1) * P],
                rhs=cod.bitcast(FP8X4),
                rhs_scale=scl,
                start=True,
                stop=True,
            )

        def project(s):
            h, g = s // G, s % G
            bank = psum.tile([P, 4, P], F32, name="acc", bufs=ACC)
            kbank[s] = bank
            for t in range(4):
                mm(bank[:, t, :], g, t, wk_cod[:, h, :], wk_scl[:, h, :])
            if MODES[s] == "A":
                for f in range(2):
                    bank = psum.tile([P, 4, P], F32, name="acc", bufs=ACC)
                    vbank[s, f] = bank
                    for t in range(4):
                        cols = slice(f * P, (f + 1) * P)
                        mm(bank[:, t, :], g, t, wv_cod[:, h, cols], wv_scl[:, h, cols])
            else:
                for f in range(2):
                    if ACS:
                        bank = psum.tile([P, 2, DV], F32, name="acs", bufs=ACS)
                    else:
                        bank = psum.tile([P, 2, DV], F32, name="acc", bufs=ACC)
                    vbank[s, f] = bank
                    for i in range(2):
                        mm(bank[:, i, :], g, 2 * f + i, wv_cod[:, h, :], wv_scl[:, h, :])

        kin = {}
        vin = {}
        vt = {}
        kcod = {}
        vcod = {}

        def ins(s):
            if s // 2 not in kin:
                k_in = stage.tile([P, 2, DK, 4], BF16, name="k_in", align_bytes=64)
                v_in = stage.tile([P, 2, DV, 4], BF16, name="v_in", align_bytes=64)
                kin[s // 2] = k_in
                vin[s // 2] = v_in

        def key(s):
            h, g = s // G, s % G
            ins(s)
            nc.vector.scalar_tensor_tensor(
                out=kin[s // 2][:, s % 2, :, :],
                in0=kbank.pop(s)[:].rearrange("p t n -> p n t"),
                scalar=0.0,
                in1=kp[:, g, h, :].unsqueeze(1).to_broadcast([P, DK, 4]),
                op0=ALU.max,
                op1=ALU.mult,
            )

        def val_direct(s):
            h, g = s // G, s % G
            ins(s)
            for f in range(2):
                nc.vector.tensor_tensor(
                    out=vin[s // 2][:, s % 2, f * P : (f + 1) * P, :],
                    in0=vbank.pop((s, f))[:].rearrange("p t n -> p n t"),
                    in1=wr[:, g, h, :].unsqueeze(1).to_broadcast([P, P, 4]),
                    op=ALU.mult,
                )

        def val_scalar(s):
            h, g = s // G, s % G
            v_t = stage.tile([P, 4, DV], BF16, name="v_t", align_bytes=64)
            vt[s] = v_t
            for t in range(4):
                nc.scalar.activation(
                    out=v_t[:, t, :] if MODES[s] != "P" else v_t[:].rearrange("p t n -> p (t n)").rearrange("p (q n e) -> p q n e", q=2, e=2)[:, t // 2, :, t % 2],
                    in_=vbank[s, t // 2][:, t % 2, :], func=COPY, scale=wr[:, g, h, t : t + 1]
                )

        def val_group(s):
            ins(s)
            if MODES[s] == "P":
                src = vt.pop(s)[:].rearrange("p t n -> p (t n)").bitcast(F32).rearrange("p (q n) -> p n q", q=2)
                dst = vin[s // 2][:, s % 2, :, :].bitcast(F32)
                if PG and s % PG == 0:
                    nc.gpsimd.tensor_scalar(out=dst, in0=src, scalar1=1.0, scalar2=0.0, op0=ALU.mult, op1=ALU.add)
                else:
                    nc.vector.tensor_copy(out=dst, in_=src)
                return
            interleave("g" if MODES[s] == "G" else "v", vin[s // 2][:, s % 2, :, :], vt.pop(s)[:])

        wbank = {}

        def weave(s):
            bank = psum.tile([P, DV, 4], BF16, name="w_acc", bufs=WB)
            wbank[s] = bank
            src = vt.pop(s)[:]
            dst = bank[:].rearrange("p n t -> p t n")
            for f in range(2):
                cols = slice(2 * f, 2 * f + 2)
                nc.tensor.matmul(out=dst[:, cols, :], lhsT=ident_b[:], rhs=src[:, cols, :], start=True, stop=True)

        def weave_out(s):
            ins(s)
            nc.scalar.copy(out=vin[s // 2][:, s % 2, :, :], in_=wbank.pop(s)[:])

        def quant_kv(p):
            kc = stage.tile([P, 2, DK], U32, name="k_cod", bufs=5, align_bytes=64)
            ks = stage.tile([P, 2, DK], U8, name="k_scl", bufs=5, align_bytes=64)
            vc = stage.tile([P, 2, DV], U32, name="v_cod", bufs=5, align_bytes=64)
            vs = stage.tile([P, 2, DV], U8, name="v_scl", bufs=5, align_bytes=64)
            kcod[p] = (kc, ks)
            vcod[p] = (vc, vs)
            nc.vector.quantize_mx(
                out=kc[:].rearrange("p a n -> p (a n)").bitcast(FP8X4),
                scales=ks[:].rearrange("p a n -> p (a n)"),
                in_=kin.pop(p)[:].rearrange("p a n t -> p (a n t)"),
            )
            nc.vector.quantize_mx(
                out=vc[:].rearrange("p a n -> p (a n)").bitcast(FP8X4),
                scales=vs[:].rearrange("p a n -> p (a n)"),
                in_=vin.pop(p)[:].rearrange("p a n t -> p (a n t)"),
            )

        obank = {}

        def fold(h):
            bank = psum.tile([P, DV], F32, name="o_acc", bufs=OB)
            obank[h] = bank
            for g in range(G):
                (kc, ks), (vc, vs) = kcod[2 * h + g // 2], vcod[2 * h + g // 2]
                nc.tensor.matmul_mx(
                    out=bank[:],
                    lhsT=kc[:, g % 2, :].bitcast(FP8X4),
                    lhsT_scale=ks[:, g % 2, :],
                    rhs=vc[:, g % 2, :].bitcast(FP8X4),
                    rhs_scale=vs[:, g % 2, :],
                    start=(g == 0),
                    stop=(g == G - 1),
                )

        def store(h):
            o = stage.tile([P, DV], F32, name="o_sb", bufs=2)
            nc.scalar.copy(out=o[:], in_=obank.pop(h)[:])
            nc.sync.dma_start(out=out[h], in_=o[:])

        def hold(p):
            mark = stage.tile([P, 1], U32, name="mark", bufs=2)
            nc.gpsimd.tensor_copy(out=mark[:], in_=vcod[p][0][:, 1, DV - 1 : DV])

        PAIRS = UNITS // 2
        if WARM:
            bank = psum.tile([P, 512], F32, name="o_acc", bufs=OB)
            for i in range(WARM):
                nc.tensor.matmul(out=bank[:], lhsT=zero[:, :P], rhs=zero[:], start=True, stop=True)

        def scales():
            nc.vector.tensor_copy(out=wr[:], in_=wr_raw[:].rearrange("p g (t h) -> p g h t", t=4))
            nc.vector.tensor_copy(out=kp[:], in_=kp_raw[:].rearrange("p g (t h) -> p g h t", t=4))

        for item in HEAD:
            f = item.split(":")
            i = int(f[1])
            if f[0] == "wd":
                widen(i, i + 1, range(4), f[2])
            elif f[0] == "iv":
                group_wv(i, i + 1, f[2])
            elif f[0] == "ik":
                group_wk(i, i + 1, f[2])
            elif f[0] == "qv":
                quant_wv(i, i + 1)
            elif f[0] == "qk":
                quant_wk(i, i + 1)
            elif f[0] == "t":
                transpose_c(i)
            elif f[0] == "o":
                c_out(i, f[2])
            elif f[0] == "q":
                quant_c(i)
            elif f[0] == "cv":
                scales()
            elif f[0] == "p":
                project(i)
            elif f[0] == "s":
                if MODES[i] != "A":
                    val_scalar(i)
            elif f[0] == "k":
                key(i)
            elif f[0] == "a":
                if MODES[i] == "A":
                    val_direct(i)
            elif f[0] == "g":
                if MODES[i] in "VPG":
                    val_group(i)
            elif f[0] == "z":
                quant_kv(i)

        for p in range(2, PAIRS + 8):
            u = p - LF
            if 0 <= u < PAIRS and u % 2 == 1:
                fold(u // 2)
            gjobs = []
            if 1 <= p - LQ < PAIRS:
                quant_kv(p - LQ)
            for a in range(HW, H):
                first = 2 * a - LEAD
                b = a + 1
                if p == max(2, first):
                    widen(a, b, range(4), WID_ENG)
                    group_wk(a, b, WK_ENG)
                if p == max(2, first + 1):
                    if WV_ENG == "g":
                        gjobs.append((group_wv, a, b))
                    else:
                        group_wv(a, b, WV_ENG)
                    quant_wk(a, b)
                if p == max(2, first + 2):
                    quant_wv(a, b)
            if 1 <= p - 1 < PAIRS:
                for s in (2 * (p - 1), 2 * (p - 1) + 1):
                    if MODES[s] in "VP":
                        val_group(s)
                    elif MODES[s] == "G":
                        gjobs.append((val_group, s))
            if gjobs and 1 <= p - LQ < PAIRS:
                hold(p - LQ)
            for job in gjobs:
                if job[0] is val_group:
                    val_group(job[1])
                else:
                    job[0](job[1], job[2], "g")
            if p < PAIRS:
                for s in (2 * p, 2 * p + 1):
                    project(s)
                    if MODES[s] != "A":
                        val_scalar(s)
                if KKAA:
                    key(2 * p)
                    key(2 * p + 1)
                    for s in (2 * p, 2 * p + 1):
                        if MODES[s] == "A":
                            val_direct(s)
                else:
                    for s in (2 * p, 2 * p + 1):
                        key(s)
                        if MODES[s] == "A":
                            val_direct(s)
            u = p - LF - LO
            if 0 <= u < PAIRS and u % 2 == 1:
                store(u // 2)
